import numpy as np, ml_dtypes
CORES = [1,2,5,6,25,26,29,30]
N = 8
ROOT = 6
def setup_inputs(rng):
    return {"x": rng.standard_normal((N, 128, 8), dtype=np.float32).astype(ml_dtypes.bfloat16)}
def reference(x):
    y = np.full((N, 128, N * 8), np.nan, x.dtype)
    y[ROOT] = np.concatenate(list(x), axis=1)
    return {"y": y}

W = 8

SCRATCH = {
    "land": ("sbuf", [128, 64], "bfloat16"),
}
SEMAPHORES = ["loaded", "arrived", "sent", "stored"]


def _engines(mask):
    return bin(mask).count("1")


def rank_program(g, core, T, topo):
    rank = T.rank_of(core)
    if rank is None:
        return
    cores = list(T.cores)
    root = cores[T.root]

    relay_of = {}
    for c in cores:
        if c != root and not topo.may_write(c, root):
            relay_of[c] = [d for d in cores
                           if topo.chip(d) == topo.chip(c) and topo.die(d) == topo.die(c)
                           and topo.may_write(d, root)][0]

    def send(dst, lo, hi):
        rid, pid, _se = topo.addr(dst)
        m = topo.mask(core, dst)
        g.remote_dma(T.land[:, lo:hi], T.land[:, lo:hi], T.sem.arrived, T.sem.sent, pid, rid, m)
        g.wait_ge(T.sem.sent, _engines(m))

    g.sync.dma_start(T.land[:, rank * W:(rank + 1) * W], T.x[:]).then_inc(T.sem.loaded, 16)
    g.wait_ge(T.sem.loaded, 16)

    if core == root:
        due = sum(_engines(topo.mask(c, root)) for c in cores if c != root and c not in relay_of)
        g.wait_ge(T.sem.arrived, due)
        g.dma_start(T.y[:], T.land[:]).then_inc(T.sem.stored, 16)
        g.wait_ge(T.sem.stored, 16)
        return

    if core in relay_of:
        send(relay_of[core], rank * W, (rank + 1) * W)
        return

    mine = [c for c in cores if relay_of.get(c) == core]
    if mine:
        g.wait_ge(T.sem.arrived, sum(_engines(topo.mask(c, core)) for c in mine))
    ranks = sorted([rank] + [cores.index(c) for c in mine])
    send(root, ranks[0] * W, (ranks[-1] + 1) * W)
